import numpy as np
import ml_dtypes


def mxq(x, axis, fmt="e4m3"):
    dtype, down = {"e4m3": (ml_dtypes.float8_e4m3fn, 7), "e5m2": (ml_dtypes.float8_e5m2, 14)}[fmt]
    v = np.moveaxis(np.asarray(x, np.float32).astype(ml_dtypes.bfloat16).astype(np.float64), axis, -1)
    blocks = v.reshape(v.shape[:-1] + (-1, 32))
    amax = np.abs(blocks).max(-1, keepdims=True)
    byte = np.maximum(np.where(amax > 0, np.frexp(amax)[1] - 1 + 127, 0) - down, 1)
    scale = np.exp2(byte - 127.0)
    codes = (blocks / scale).astype(np.float32).astype(dtype).astype(np.float64)
    return np.moveaxis((codes * scale).reshape(v.shape), -1, axis)


WIDE = False


def mx_kscale(k):
    if not WIDE:
        return np.ones(k)
    levels = np.array([10, -10, 5, -5, 0])
    if k % 512:
        return np.exp2(np.random.permutation(np.resize(levels, k // 32))).repeat(32)
    a = np.empty((k // 512, 16))
    for p in range(k // 512):
        a[p, :8] = np.random.permutation(np.resize(levels, 8))
        for g in range(8):
            far = levels[np.abs(levels - a[p, g]) >= 10]
            a[p, g + 8] = far[np.random.randint(len(far))]
    return np.exp2(a.ravel()).repeat(32)


def f64(x):
    return np.asarray(x).astype(np.float64)


def striped(idx):
    return np.tile(idx.reshape(-1, 16).T, (8, 1)).astype(np.uint16)


def unstriped(offs):
    return offs[:16].T.reshape(-1).astype(np.int64)


def striped8(idx):
    return np.concatenate([x.reshape(-1, 16).T for x in idx]).astype(np.uint16)


def runs(offs, k):
    lists = np.stack([offs[16 * r : 16 * r + 16].T.reshape(-1) for r in range(8)]).astype(np.int64)
    return lists[np.arange(k) % 512 // 64]


def pack_weight(w):
    k, n = w.shape
    w = f64(np.asarray(w, np.float32).astype(ml_dtypes.bfloat16)).reshape(k // 32, 32, n)
    amax = np.abs(w).max(1)
    byte = np.clip(np.where(amax > 0, np.frexp(amax)[1] - 1 + 127 - 7, 1), 1, 254)
    scaled = (w * np.exp2(127.0 - byte)[:, None, :]).reshape(k, n).astype(np.float32)
    words = np.ascontiguousarray(scaled.reshape(k // 512, 128, 4, n).transpose(0, 1, 3, 2)).astype(ml_dtypes.float8_e4m3fn).view(np.uint8)
    return words, np.ascontiguousarray(byte.astype(np.uint8).reshape(k // 512, 16, n))


def unpack_weight(words, scales):
    g, p, n, _ = words.shape
    vals = np.ascontiguousarray(words).view(ml_dtypes.float8_e4m3fn).astype(np.float64) * np.repeat(np.exp2(scales.astype(np.float64) - 127.0), 8, axis=1)[..., None]
    return vals.transpose(0, 1, 3, 2).reshape(g * 512, n)


K, T, S, N, H = 512, 2048, 512, 512, 512


def setup_inputs():
    n = np.random.standard_normal
    s = mx_kscale(K)[:, None]
    u = mx_kscale(H)
    packed_xT = pack_weight(n((K, T)) * s)
    return {
        "x_words": packed_xT[0],
        "x_scales": packed_xT[1],
        "w1": (n((K, H)) / np.sqrt(K) / s).astype(np.float32),
        "gn": (np.random.uniform(0.5, 1.5, (H, 1)) * u[:, None]).astype(np.float32),
        "w2": (n((H, N)) / np.sqrt(H) / u[:, None]).astype(np.float32),
        "gm": (np.random.uniform(0.5, 1.5, (H, 1)) * u[:, None]).astype(np.float32),
        "w3": (n((H, N)) / np.sqrt(H) / u[:, None]).astype(np.float32),
        "offs": striped(np.random.permutation(T)[:S]),
        "n1": striped8(np.stack([np.random.permutation(S) for _ in range(8)])),
        "n2": striped8(np.stack([np.random.permutation(S) for _ in range(8)])),
        "n3": striped8(np.stack([np.random.permutation(S) for _ in range(8)])),
        "n4": striped8(np.stack([np.random.permutation(S) for _ in range(8)])),
        "n5": striped8(np.stack([np.random.permutation(S) for _ in range(8)])),
        "n6": striped8(np.stack([np.random.permutation(S) for _ in range(8)])),
    }


def reference(x_words, x_scales, w1, gn, w2, gm, w3, offs, n1, n2, n3, n4, n5, n6):
    xq = unpack_weight(x_words, x_scales)[:, unstriped(offs)]
    y = mxq(f64(w1), 0, "e4m3").T @ xq
    z = f64(gn) * (y * (y[np.arange(H)[:, None], runs(n1, H)] - (y[np.arange(H)[:, None], runs(n2, H)])))
    a = mxq(f64(w2), 0, "e4m3").T @ mxq(z, 0, "e4m3")
    st = np.maximum(y, y[np.arange(H)[:, None], runs(n3, H)])
    z2 = f64(gm) * (st[np.arange(H)[:, None], runs(n4, H)] - (0.5 * y))
    b = mxq(f64(w3), 0, "e4m3").T @ mxq(z2, 0, "e4m3")
    return (a - (a[np.arange(N)[:, None], runs(n5, N)])) / (np.abs(b) + np.abs(b[np.arange(N)[:, None], runs(n6, N)]) + 0.5)

@@ -1,0 +1,178 @@
+from contextlib import ExitStack
+
+import concourse.mybir as mybir
+
+K, T, S, H, N = 512, 2048, 512, 512, 512
+FLOPS = 2 * K * H * S + 2 * 2 * H * N * S
+
+F32 = mybir.dt.float32
+BF16 = mybir.dt.bfloat16
+I32 = mybir.dt.int32
+U32 = mybir.dt.uint32
+U16 = mybir.dt.uint16
+U8 = mybir.dt.uint8
+FP8X4 = mybir.dt.float8_e4m3fn_x4
+ALU = mybir.AluOpType
+ACT = mybir.ActivationFunctionType
+
+P = 128
+PACK = 4
+WIN = 2 * S
+
+
+def tile_picked_forknormbwindhopb_none_p_kernel(tc, x_words, x_scales, w1, gn, w2, gm, w3, offs, n1, n2, n3, n4, n5, n6, out):
+    nc = tc.nc
+    planes = range(PACK)
+    with ExitStack() as ctx:
+        keep = ctx.enter_context(tc.tile_pool(name="keep", bufs=1))
+        psum = ctx.enter_context(tc.psum_pool(name="psum", bufs=1))
+
+        def tile(name, shape, dtype):
+            return keep.tile(shape, dtype, name=name, align_bytes=64)
+
+        def load_list(name, src):
+            dst = tile(name, [P, S // 16], U16)
+            nc.sync.dma_start(dst[:], src)
+            return dst
+
+        def load_rows(name, w, c0, c1):
+            raw = tile(name, [P, PACK, c1 - c0], F32)
+            nc.sync.dma_start(out=raw[:], in_=w.rearrange("(p j) c -> p j c", j=PACK)[:, :, c0:c1])
+            return raw
+
+        def load_gain(name, g):
+            dst = tile(name, [P, PACK], F32)
+            nc.sync.dma_start(out=dst[:], in_=g.rearrange("(p t) o -> p (t o)", t=PACK))
+            return dst
+
+        def deal(copy, grouped, raw, m0):
+            m = raw.shape[2] // PACK
+            copy(grouped[:].rearrange("p (t m j) -> p m j t", t=PACK, j=PACK)[:, m0 : m0 + m],
+                 raw[:].rearrange("p j (m t) -> p m j t", t=PACK))
+
+        def quantize(name, grouped):
+            codes = tile(name + "_codes", [P, S], U32)
+            scales = tile(name + "_scales", [P, S], U8)
+            nc.vector.quantize_mx(out=codes[:].bitcast(FP8X4), scales=scales[:], in_=grouped[:])
+            return codes, scales
+
+        def product(bank, weights, acts, t):
+            cols = slice(P * t, P * (t + 1))
+            nc.tensor.matmul_mx(out=bank[:], lhsT=weights[0][:, cols].bitcast(FP8X4), lhsT_scale=weights[1][:, cols],
+                                rhs=acts[0][:].bitcast(FP8X4), rhs_scale=acts[1][:], start=True, stop=True)
+
+        def woven(grouped):
+            return grouped[:].rearrange("p (c i t) -> p c t i", i=4, t=PACK)
+
+        def unwoven(rows):
+            return rows[:].rearrange("p t (c i) -> p c t i", i=4)
+
+        one = tile("one", [P, 1], F32)
+        nc.vector.memset(one[:], 1.0)
+        warm = tile("warm", [P, 1], F32)
+        nc.scalar.activation(warm[:], one[:], ACT.Ln)
+
+        xs_all = tile("xs_all", [P, T], U8)
+        nc.vector.memset(xs_all[:].bitcast(I32), 0)
+        w1_lo = load_rows("w1_lo", w1, 0, H // 2)
+        for q in range(4):
+            nc.sync.dma_start(out=xs_all[32 * q : 32 * q + 4, :].bitcast(I32), in_=x_scales[0, 4 * q : 4 * q + 4, :].bitcast(I32))
+        offs_t = load_list("offs_t", offs)
+        w1_hi = load_rows("w1_hi", w1, H // 2, H)
+        xw_all = tile("xw_all", [P, T], U32)
+        nc.sync.dma_start(out=xw_all[:].bitcast(I32), in_=x_words[0].rearrange("p c r -> p (c r)").bitcast(I32))
+        n3_t = load_list("n3_t", n3)
+        n4_t = load_list("n4_t", n4)
+        gm_t = load_gain("gm_t", gm)
+        gn_t = load_gain("gn_t", gn)
+        w3_raw = load_rows("w3_raw", w3, 0, N)
+        n2_t = load_list("n2_t", n2)
+        n1_t = load_list("n1_t", n1)
+        w2_raw = load_rows("w2_raw", w2, 0, N)
+        n6_t = load_list("n6_t", n6)
+        n5_t = load_list("n5_t", n5)
+
+        w1_g = tile("w1_g", [P, PACK * H], BF16)
+        deal(nc.scalar.copy, w1_g, w1_lo, 0)
+        deal(nc.vector.tensor_copy, w1_g, w1_hi, P // 2)
+        xs = tile("xs", [P, S], U8)
+        nc.vector.tensor_copy(xs[:], xs_all[:].indirect(offs_t[:]))
+        w1_q = quantize("w1", w1_g)
+        xw = tile("xw", [P, S], U32)
+        nc.vector.tensor_copy(xw[:], xw_all[:].indirect(offs_t[:]))
+
+        y_bank = [psum.tile([P, S], F32, name="y_bank%d" % t, tag="ya%d" % t) for t in planes]
+        y = [tile("y%d" % t, [P, WIN], F32) for t in planes]
+        for t in planes:
+            product(y_bank[t], w1_q, (xw, xs), t)
+            nc.scalar.copy(y[t][:, :S], y_bank[t][:])
+        half_y = tile("half_y", [P, PACK, S], F32)
+        for t in planes:
+            nc.scalar.activation(half_y[:, t, :], y_bank[t][:], ACT.Copy, scale=0.5)
+        w3_g = tile("w3_g", [P, PACK * N], BF16)
+        deal(nc.scalar.copy, w3_g, w3_raw, 0)
+
+        st = [tile("st%d" % t, [P, WIN], F32) for t in planes]
+        for t in planes:
+            nc.vector.tensor_copy(st[t][:, S:], y[t][:].indirect(n3_t[:]))
+        for t in planes:
+            nc.vector.tensor_tensor(st[t][:, :S], st[t][:, S:], y[t][:, :S], ALU.max)
+        u = tile("u", [P, PACK, S], F32)
+        z2_rows = tile("z2_rows", [P, PACK, S], BF16)
+        for t in planes:
+            nc.vector.tensor_tensor(u[:, t, :], st[t][:].indirect(n4_t[:]), half_y[:, t, :], ALU.subtract)
+            nc.scalar.activation(z2_rows[:, t, :], u[:, t, :], ACT.Copy, scale=gm_t[:, t : t + 1])
+        z2_g = tile("z2_g", [P, PACK * S], BF16)
+        nc.scalar.copy(woven(z2_g), unwoven(z2_rows))
+        w3_q = quantize("w3", w3_g)
+
+        gain_y = tile("gain_y", [P, PACK, S], F32)
+        for t in planes:
+            nc.scalar.activation(gain_y[:, t, :], y_bank[t][:], ACT.Copy, scale=gn_t[:, t : t + 1])
+        w2_g = tile("w2_g", [P, PACK * N], BF16)
+        deal(nc.scalar.copy, w2_g, w2_raw, 0)
+
+        y_n2 = tile("y_n2", [P, PACK, S], F32)
+        for t in planes:
+            nc.vector.tensor_copy(y_n2[:, t, :], y[t][:].indirect(n2_t[:]))
+        z2_q = quantize("z2", z2_g)
+        b_bank = [psum.tile([P, S], F32, name="b_bank%d" % t, tag="b%d" % t) for t in planes]
+        size_b = [tile("size_b%d" % t, [P, WIN], F32) for t in planes]
+        size_own = tile("size_own", [P, PACK, S], F32)
+        for t in planes:
+            product(b_bank[t], w3_q, z2_q, t)
+            nc.scalar.activation(size_b[t][:, :S], b_bank[t][:], ACT.Abs)
+            nc.scalar.activation(size_own[:, t, :], b_bank[t][:], ACT.Abs)
+
+        diff = tile("diff", [P, PACK, S], F32)
+        for t in planes:
+            nc.vector.tensor_tensor(diff[:, t, :], y[t][:].indirect(n1_t[:]), y_n2[:, t, :], ALU.subtract)
+        w2_q = quantize("w2", w2_g)
+        z_g = tile("z_g", [P, PACK * S], BF16)
+        nc.vector.tensor_tensor(woven(z_g), unwoven(diff), unwoven(gain_y), ALU.mult)
+        den = tile("den", [P, PACK, S], F32)
+        nc.vector.tensor_tensor(den[:, 0, :], size_b[0][:].indirect(n6_t[:]), size_own[:, 0, :], ALU.add)
+        z_q = quantize("z", z_g)
+        a_bank = [psum.tile([P, S], F32, name="a_bank%d" % t, tag="ya%d" % t) for t in planes]
+        minus_a = [tile("minus_a%d" % t, [P, WIN], F32) for t in planes]
+        a_own = tile("a_own", [P, PACK, S], F32)
+        for t in planes:
+            product(a_bank[t], w2_q, z_q, t)
+            nc.scalar.activation(minus_a[t][:, :S], a_bank[t][:], ACT.Copy, scale=-1.0)
+            nc.scalar.copy(a_own[:, t, :], a_bank[t][:])
+        for t in planes[1:]:
+            nc.vector.tensor_tensor(den[:, t, :], size_b[t][:].indirect(n6_t[:]), size_own[:, t, :], ALU.add)
+        log_den = tile("log_den", [P, PACK, S], F32)
+        nc.scalar.activation(log_den[:], den[:], ACT.Ln, bias=0.5)
+        inv_den = tile("inv_den", [P, PACK, S], F32)
+        for t in planes:
+            nc.scalar.activation(inv_den[:, t, :], log_den[:, t, :], ACT.Exp, scale=-1.0)
+
+        num = tile("num", [P, PACK, S], F32)
+        res = tile("res", [P, PACK, S], F32)
+        out_rows = out.rearrange("(p t) s -> p t s", t=PACK)
+        for t in planes:
+            nc.vector.tensor_tensor(num[:, t, :], minus_a[t][:].indirect(n5_t[:]), a_own[:, t, :], ALU.add)
+        for t in planes:
+            nc.vector.tensor_tensor(res[:, t, :], num[:, t, :], inv_den[:, t, :], ALU.mult)
+            nc.sync.dma_start(out=out_rows[:, t, :], in_=res[:, t, :])

@@ -27,8 +27,8 @@ def tile_picked_forknormbwindhopb_none_p_kernel(tc, x_words, x_scales, w1, gn, w
         keep = ctx.enter_context(tc.tile_pool(name="keep", bufs=1))
         psum = ctx.enter_context(tc.psum_pool(name="psum", bufs=1))
 
-        def tile(name, shape, dtype):
-            return keep.tile(shape, dtype, name=name, align_bytes=64)
+        def tile(name, shape, dtype, tag=None):
+            return keep.tile(shape, dtype, name=name, tag=tag or name, align_bytes=64)
 
         def load_list(name, src):
             dst = tile(name, [P, S // 16], U16)
@@ -56,10 +56,10 @@ def tile_picked_forknormbwindhopb_none_p_kernel(tc, x_words, x_scales, w1, gn, w
             nc.vector.quantize_mx(out=codes[:].bitcast(FP8X4), scales=scales[:], in_=grouped[:])
             return codes, scales
 
-        def product(bank, weights, acts, t):
+        def product(bank, weights, acts, t, places=slice(0, S)):
             cols = slice(P * t, P * (t + 1))
-            nc.tensor.matmul_mx(out=bank[:], lhsT=weights[0][:, cols].bitcast(FP8X4), lhsT_scale=weights[1][:, cols],
-                                rhs=acts[0][:].bitcast(FP8X4), rhs_scale=acts[1][:], start=True, stop=True)
+            nc.tensor.matmul_mx(out=bank[:, places], lhsT=weights[0][:, cols].bitcast(FP8X4), lhsT_scale=weights[1][:, cols],
+                                rhs=acts[0][:, places].bitcast(FP8X4), rhs_scale=acts[1][:, places], start=True, stop=True)
 
         def woven(grouped):
             return grouped[:].rearrange("p (c i t) -> p c t i", i=4, t=PACK)
@@ -99,12 +99,15 @@ def tile_picked_forknormbwindhopb_none_p_kernel(tc, x_words, x_scales, w1, gn, w
         nc.vector.tensor_copy(xs[:], xs_all[:].indirect(offs_t[:]))
         w1_q = quantize("w1", w1_g)
         xw = tile("xw", [P, S], U32)
-        nc.vector.tensor_copy(xw[:], xw_all[:].indirect(offs_t[:]))
+        halves = [slice(0, S // 2), slice(S // 2, S)]
+        for h in range(2):
+            nc.vector.tensor_copy(xw[:, halves[h]], xw_all[:].indirect(offs_t[:, 16 * h : 16 * (h + 1)]))
 
         y_bank = [psum.tile([P, S], F32, name="y_bank%d" % t, tag="ya%d" % t) for t in planes]
         y = [tile("y%d" % t, [P, WIN], F32) for t in planes]
         for t in planes:
-            product(y_bank[t], w1_q, (xw, xs), t)
+            product(y_bank[t], w1_q, (xw, xs), t, halves[0])
+            product(y_bank[t], w1_q, (xw, xs), t, halves[1])
             nc.scalar.copy(y[t][:, :S], y_bank[t][:])
         half_y = tile("half_y", [P, PACK, S], F32)
         for t in planes:
@@ -116,23 +119,23 @@ def tile_picked_forknormbwindhopb_none_p_kernel(tc, x_words, x_scales, w1, gn, w
         for t in planes:
             nc.vector.tensor_copy(st[t][:, S:], y[t][:].indirect(n3_t[:]))
         for t in planes:
-            nc.vector.tensor_tensor(st[t][:, :S], st[t][:, S:], y[t][:, :S], ALU.max)
+            nc.vector.tensor_tensor(st[t][:, :S], st[t][:, S:], y_bank[t][:], ALU.max)
+        gain_y = tile("gain_y", [P, PACK, S], F32)
+        for t in planes:
+            nc.scalar.activation(gain_y[:, t, :], y_bank[t][:], ACT.Copy, scale=gn_t[:, t : t + 1])
         u = tile("u", [P, PACK, S], F32)
         z2_rows = tile("z2_rows", [P, PACK, S], BF16)
         for t in planes:
             nc.vector.tensor_tensor(u[:, t, :], st[t][:].indirect(n4_t[:]), half_y[:, t, :], ALU.subtract)
             nc.scalar.activation(z2_rows[:, t, :], u[:, t, :], ACT.Copy, scale=gm_t[:, t : t + 1])
-        z2_g = tile("z2_g", [P, PACK * S], BF16)
+        z2_g = tile("z2_g", [P, PACK * S], BF16, tag="z2_then_diff")
         nc.scalar.copy(woven(z2_g), unwoven(z2_rows))
         w3_q = quantize("w3", w3_g)
 
-        gain_y = tile("gain_y", [P, PACK, S], F32)
-        for t in planes:
-            nc.scalar.activation(gain_y[:, t, :], y_bank[t][:], ACT.Copy, scale=gn_t[:, t : t + 1])
         w2_g = tile("w2_g", [P, PACK * N], BF16)
         deal(nc.scalar.copy, w2_g, w2_raw, 0)
 
-        y_n2 = tile("y_n2", [P, PACK, S], F32)
+        y_n2 = half_y
         for t in planes:
             nc.vector.tensor_copy(y_n2[:, t, :], y[t][:].indirect(n2_t[:]))
         z2_q = quantize("z2", z2_g)
@@ -142,16 +145,14 @@ def tile_picked_forknormbwindhopb_none_p_kernel(tc, x_words, x_scales, w1, gn, w
         for t in planes:
             product(b_bank[t], w3_q, z2_q, t)
             nc.scalar.activation(size_b[t][:, :S], b_bank[t][:], ACT.Abs)
-            nc.scalar.activation(size_own[:, t, :], b_bank[t][:], ACT.Abs)
+            nc.sync.dma_start(out=size_own[:, t, :], in_=size_b[t][:, :S])
 
-        diff = tile("diff", [P, PACK, S], F32)
+        diff = tile("diff", [P, PACK, S], F32, tag="z2_then_diff")
         for t in planes:
             nc.vector.tensor_tensor(diff[:, t, :], y[t][:].indirect(n1_t[:]), y_n2[:, t, :], ALU.subtract)
         w2_q = quantize("w2", w2_g)
         z_g = tile("z_g", [P, PACK * S], BF16)
         nc.vector.tensor_tensor(woven(z_g), unwoven(diff), unwoven(gain_y), ALU.mult)
-        den = tile("den", [P, PACK, S], F32)
-        nc.vector.tensor_tensor(den[:, 0, :], size_b[0][:].indirect(n6_t[:]), size_own[:, 0, :], ALU.add)
         z_q = quantize("z", z_g)
         a_bank = [psum.tile([P, S], F32, name="a_bank%d" % t, tag="ya%d" % t) for t in planes]
         minus_a = [tile("minus_a%d" % t, [P, WIN], F32) for t in planes]
@@ -159,20 +160,32 @@ def tile_picked_forknormbwindhopb_none_p_kernel(tc, x_words, x_scales, w1, gn, w
         for t in planes:
             product(a_bank[t], w2_q, z_q, t)
             nc.scalar.activation(minus_a[t][:, :S], a_bank[t][:], ACT.Copy, scale=-1.0)
-            nc.scalar.copy(a_own[:, t, :], a_bank[t][:])
-        for t in planes[1:]:
-            nc.vector.tensor_tensor(den[:, t, :], size_b[t][:].indirect(n6_t[:]), size_own[:, t, :], ALU.add)
+            nc.sync.dma_start(out=a_own[:, t, :], in_=minus_a[t][:, :S])
+        den = tile("den", [P, PACK, S], F32)
         log_den = tile("log_den", [P, PACK, S], F32)
-        nc.scalar.activation(log_den[:], den[:], ACT.Ln, bias=0.5)
-        inv_den = tile("inv_den", [P, PACK, S], F32)
         for t in planes:
-            nc.scalar.activation(inv_den[:, t, :], log_den[:, t, :], ACT.Exp, scale=-1.0)
+            nc.vector.tensor_tensor(den[:, t, :], size_b[t][:].indirect(n6_t[:]), size_own[:, t, :], ALU.add)
+            nc.scalar.activation(log_den[:, t, :], den[:, t, :], ACT.Ln, bias=0.5)
+        inv_den = [den[:, PACK - 1, :]] + [log_den[:, t, :] for t in planes[:-1]]
+        for t in planes:
+            nc.scalar.activation(inv_den[t], log_den[:, t, :], ACT.Exp, scale=-1.0)
 
-        num = tile("num", [P, PACK, S], F32)
+        num = tile("num", [P, PACK - 1, S], F32)
         res = tile("res", [P, PACK, S], F32)
         out_rows = out.rearrange("(p t) s -> p t s", t=PACK)
-        for t in planes:
-            nc.vector.tensor_tensor(num[:, t, :], minus_a[t][:].indirect(n5_t[:]), a_own[:, t, :], ALU.add)
-        for t in planes:
-            nc.vector.tensor_tensor(res[:, t, :], num[:, t, :], inv_den[:, t, :], ALU.mult)
-            nc.sync.dma_start(out=out_rows[:, t, :], in_=res[:, t, :])
+
+        def numerator(t):
+            nc.vector.tensor_tensor(num[:, t % 3, :], minus_a[t][:].indirect(n5_t[:]), a_own[:, t, :], ALU.subtract)
+
+        def finish(t, places):
+            nc.vector.tensor_tensor(res[:, t, places], num[:, t % 3, places], inv_den[t][:, places], ALU.mult)
+            nc.sync.dma_start(out=out_rows[:, t, places], in_=res[:, t, places])
+
+        for t in range(3):
+            numerator(t)
+        finish(0, slice(0, S))
+        finish(1, slice(0, S))
+        numerator(3)
+        finish(2, slice(0, S))
+        finish(3, halves[0])
+        finish(3, halves[1])

@@ -50,22 +50,27 @@ def tile_picked_forknormbwindhopb_none_p_kernel(tc, x_words, x_scales, w1, gn, w
             copy(grouped[:].rearrange("p (t m j) -> p m j t", t=PACK, j=PACK)[:, m0 : m0 + m],
                  raw[:].rearrange("p j (m t) -> p m j t", t=PACK))
 
+        def mx_tiles(name):
+            return tile(name + "_codes", [P, S], U32), tile(name + "_scales", [P, S], U8)
+
+        def quantize_part(q, cols, grouped):
+            nc.vector.quantize_mx(out=q[0][:, cols].bitcast(FP8X4), scales=q[1][:, cols], in_=grouped)
+
         def quantize(name, grouped):
-            codes = tile(name + "_codes", [P, S], U32)
-            scales = tile(name + "_scales", [P, S], U8)
-            nc.vector.quantize_mx(out=codes[:].bitcast(FP8X4), scales=scales[:], in_=grouped[:])
-            return codes, scales
+            q = mx_tiles(name)
+            quantize_part(q, slice(0, S), grouped[:])
+            return q
 
         def product(bank, weights, acts, t, places=slice(0, S)):
             cols = slice(P * t, P * (t + 1))
             nc.tensor.matmul_mx(out=bank[:, places], lhsT=weights[0][:, cols].bitcast(FP8X4), lhsT_scale=weights[1][:, cols],
                                 rhs=acts[0][:, places].bitcast(FP8X4), rhs_scale=acts[1][:, places], start=True, stop=True)
 
-        def woven(grouped):
-            return grouped[:].rearrange("p (c i t) -> p c t i", i=4, t=PACK)
+        def woven(grouped, i):
+            return grouped.rearrange("p (c i t) -> p c t i", i=i, t=PACK)
 
-        def unwoven(rows):
-            return rows[:].rearrange("p t (c i) -> p c t i", i=4)
+        def unwoven(rows, i):
+            return rows.rearrange("p t (c i) -> p c t i", i=i)
 
         one = tile("one", [P, 1], F32)
         nc.vector.memset(one[:], 1.0)
@@ -128,8 +133,10 @@ def tile_picked_forknormbwindhopb_none_p_kernel(tc, x_words, x_scales, w1, gn, w
         for t in planes:
             nc.vector.tensor_tensor(u[:, t, :], st[t][:].indirect(n4_t[:]), half_y[:, t, :], ALU.subtract)
             nc.scalar.activation(z2_rows[:, t, :], u[:, t, :], ACT.Copy, scale=gm_t[:, t : t + 1])
-        z2_g = tile("z2_g", [P, PACK * S], BF16, tag="z2_then_diff")
-        nc.scalar.copy(woven(z2_g), unwoven(z2_rows))
+        diff = tile("diff", [P, PACK, S], F32)
+        z2_g = [diff[:, h, :].bitcast(BF16) for h in range(2)]
+        for h in range(2):
+            nc.scalar.copy(woven(z2_g[h], 4), unwoven(z2_rows[:, :, halves[h]], 4))
         w3_q = quantize("w3", w3_g)
 
         w2_g = tile("w2_g", [P, PACK * N], BF16)
@@ -138,7 +145,9 @@ def tile_picked_forknormbwindhopb_none_p_kernel(tc, x_words, x_scales, w1, gn, w
         y_n2 = half_y
         for t in planes:
             nc.vector.tensor_copy(y_n2[:, t, :], y[t][:].indirect(n2_t[:]))
-        z2_q = quantize("z2", z2_g)
+        z2_q = mx_tiles("z2")
+        for h in range(2):
+            quantize_part(z2_q, halves[h], z2_g[h])
         b_bank = [psum.tile([P, S], F32, name="b_bank%d" % t, tag="b%d" % t) for t in planes]
         size_b = [tile("size_b%d" % t, [P, WIN], F32) for t in planes]
         size_own = tile("size_own", [P, PACK, S], F32)
@@ -147,13 +156,15 @@ def tile_picked_forknormbwindhopb_none_p_kernel(tc, x_words, x_scales, w1, gn, w
             nc.scalar.activation(size_b[t][:, :S], b_bank[t][:], ACT.Abs)
             nc.sync.dma_start(out=size_own[:, t, :], in_=size_b[t][:, :S])
 
-        diff = tile("diff", [P, PACK, S], F32, tag="z2_then_diff")
         for t in planes:
             nc.vector.tensor_tensor(diff[:, t, :], y[t][:].indirect(n1_t[:]), y_n2[:, t, :], ALU.subtract)
         w2_q = quantize("w2", w2_g)
-        z_g = tile("z_g", [P, PACK * S], BF16)
-        nc.vector.tensor_tensor(woven(z_g), unwoven(diff), unwoven(gain_y), ALU.mult)
-        z_q = quantize("z", z_g)
+        z_g = [tile("z_g%d" % h, [P, PACK * S // 2], BF16) for h in range(2)]
+        z_q = mx_tiles("z")
+        for h in range(2):
+            nc.vector.tensor_tensor(woven(z_g[h][:], 2), unwoven(diff[:, :, halves[h]], 2), unwoven(gain_y[:, :, halves[h]], 2), ALU.mult)
+        for h in range(2):
+            quantize_part(z_q, halves[h], z_g[h][:])
         a_bank = [psum.tile([P, S], F32, name="a_bank%d" % t, tag="ya%d" % t) for t in planes]
         minus_a = [tile("minus_a%d" % t, [P, WIN], F32) for t in planes]
         a_own = tile("a_own", [P, PACK, S], F32)

@@ -17,12 +17,16 @@ ACT = mybir.ActivationFunctionType
 
 P = 128
 PACK = 4
+LIST_ROWS = 16
 WIN = 2 * S
+LAST = PACK - 1
 
 
 def tile_picked_forknormbwindhopb_none_p_kernel(tc, x_words, x_scales, w1, gn, w2, gm, w3, offs, n1, n2, n3, n4, n5, n6, out):
     nc = tc.nc
     planes = range(PACK)
+    whole = slice(0, S)
+    halves = [slice(0, S // 2), slice(S // 2, S)]
     with ExitStack() as ctx:
         keep = ctx.enter_context(tc.tile_pool(name="keep", bufs=1))
         psum = ctx.enter_context(tc.psum_pool(name="psum", bufs=1))
@@ -31,7 +35,7 @@ def tile_picked_forknormbwindhopb_none_p_kernel(tc, x_words, x_scales, w1, gn, w
             return keep.tile(shape, dtype, name=name, tag=tag or name, align_bytes=64)
 
         def load_list(name, src):
-            dst = tile(name, [P, S // 16], U16)
+            dst = tile(name, [P, S // LIST_ROWS], U16)
             nc.sync.dma_start(dst[:], src)
             return dst
 
@@ -53,15 +57,15 @@ def tile_picked_forknormbwindhopb_none_p_kernel(tc, x_words, x_scales, w1, gn, w
         def mx_tiles(name):
             return tile(name + "_codes", [P, S], U32), tile(name + "_scales", [P, S], U8)
 
-        def quantize_part(q, cols, grouped):
-            nc.vector.quantize_mx(out=q[0][:, cols].bitcast(FP8X4), scales=q[1][:, cols], in_=grouped)
+        def quantize_part(operand, cols, grouped):
+            nc.vector.quantize_mx(out=operand[0][:, cols].bitcast(FP8X4), scales=operand[1][:, cols], in_=grouped)
 
         def quantize(name, grouped):
-            q = mx_tiles(name)
-            quantize_part(q, slice(0, S), grouped[:])
-            return q
+            operand = mx_tiles(name)
+            quantize_part(operand, whole, grouped[:])
+            return operand
 
-        def product(bank, weights, acts, t, places=slice(0, S)):
+        def product(bank, weights, acts, t, places=whole):
             cols = slice(P * t, P * (t + 1))
             nc.tensor.matmul_mx(out=bank[:, places], lhsT=weights[0][:, cols].bitcast(FP8X4), lhsT_scale=weights[1][:, cols],
                                 rhs=acts[0][:, places].bitcast(FP8X4), rhs_scale=acts[1][:, places], start=True, stop=True)
@@ -74,8 +78,8 @@ def tile_picked_forknormbwindhopb_none_p_kernel(tc, x_words, x_scales, w1, gn, w
 
         one = tile("one", [P, 1], F32)
         nc.vector.memset(one[:], 1.0)
-        warm = tile("warm", [P, 1], F32)
-        nc.scalar.activation(warm[:], one[:], ACT.Ln)
+        log_one = tile("log_one", [P, 1], F32)
+        nc.scalar.activation(log_one[:], one[:], ACT.Ln)
 
         xs_all = tile("xs_all", [P, T], U8)
         nc.vector.memset(xs_all[:].bitcast(I32), 0)
@@ -86,12 +90,12 @@ def tile_picked_forknormbwindhopb_none_p_kernel(tc, x_words, x_scales, w1, gn, w
         w1_hi = load_rows("w1_hi", w1, H // 2, H)
         xw_all = tile("xw_all", [P, T], U32)
         nc.sync.dma_start(out=xw_all[:].bitcast(I32), in_=x_words[0].rearrange("p c r -> p (c r)").bitcast(I32))
+        n2_t = load_list("n2_t", n2)
         n3_t = load_list("n3_t", n3)
         n4_t = load_list("n4_t", n4)
         gm_t = load_gain("gm_t", gm)
         gn_t = load_gain("gn_t", gn)
         w3_raw = load_rows("w3_raw", w3, 0, N)
-        n2_t = load_list("n2_t", n2)
         n1_t = load_list("n1_t", n1)
         w2_raw = load_rows("w2_raw", w2, 0, N)
         n6_t = load_list("n6_t", n6)
@@ -104,50 +108,78 @@ def tile_picked_forknormbwindhopb_none_p_kernel(tc, x_words, x_scales, w1, gn, w
         nc.vector.tensor_copy(xs[:], xs_all[:].indirect(offs_t[:]))
         w1_q = quantize("w1", w1_g)
         xw = tile("xw", [P, S], U32)
-        halves = [slice(0, S // 2), slice(S // 2, S)]
+        half_list = S // 2 // LIST_ROWS
         for h in range(2):
-            nc.vector.tensor_copy(xw[:, halves[h]], xw_all[:].indirect(offs_t[:, 16 * h : 16 * (h + 1)]))
+            nc.vector.tensor_copy(xw[:, halves[h]], xw_all[:].indirect(offs_t[:, half_list * h : half_list * (h + 1)]))
 
         y_bank = [psum.tile([P, S], F32, name="y_bank%d" % t, tag="ya%d" % t) for t in planes]
         y = [tile("y%d" % t, [P, WIN], F32) for t in planes]
-        for t in planes:
-            product(y_bank[t], w1_q, (xw, xs), t, halves[0])
-            product(y_bank[t], w1_q, (xw, xs), t, halves[1])
-            nc.scalar.copy(y[t][:, :S], y_bank[t][:])
+        y_own = tile("y_own", [P, LAST, S], F32)
+        early_bank = psum.tile([P, S], F32, name="early_bank", tag="b%d" % LAST)
+        for h, bank in enumerate((early_bank, y_bank[0])):
+            product(bank, w1_q, (xw, xs), 0, halves[h])
+            nc.scalar.copy(y[0][:, halves[h]], bank[:, halves[h]])
+        y_src = [y[0][:, :S]] + [y_bank[t][:] for t in planes[1:]]
+        nc.scalar.copy(y_own[:, 0, :], y_src[0])
+        for t in planes[1:]:
+            product(y_bank[t], w1_q, (xw, xs), t)
+            nc.scalar.copy(y[t][:, :S], y_src[t])
+            if t < LAST:
+                nc.scalar.copy(y_own[:, t, :], y_src[t])
+
+        n4_order = (LAST, 0, 1, 2)
+        st = [tile("st%d" % t, [P, PACK * S if t == n4_order[-1] else WIN], F32) for t in planes]
+        y_n2 = tile("y_n2", [P, PACK, S], F32)
+        ungained = tile("ungained", [P, PACK, S], F32)
+        rise = ungained
+        for t in planes[:LAST]:
+            nc.vector.tensor_copy(y_n2[:, t, :], y[t][:].indirect(n2_t[:]))
+            nc.vector.tensor_tensor(st[t][:, S:WIN], y[t][:].indirect(n3_t[:]), y_own[:, t, :], ALU.subtract)
+        nc.vector.tensor_copy(st[LAST][:, S:], y[LAST][:].indirect(n3_t[:]))
+        nc.vector.tensor_copy(y_n2[:, LAST, :], y[LAST][:].indirect(n2_t[:]))
+        diff = st[n4_order[-1]][:].rearrange("p (t s) -> p t s", t=PACK)
         half_y = tile("half_y", [P, PACK, S], F32)
-        for t in planes:
-            nc.scalar.activation(half_y[:, t, :], y_bank[t][:], ACT.Copy, scale=0.5)
+
+        def larger(t):
+            nc.scalar.activation(rise[:, t, :], st[t][:, S:WIN], ACT.Relu)
+            nc.gpsimd.tensor_tensor(st[t][:, :S], rise[:, t, :], y_own[:, t, :], ALU.add)
+
+        def halve(t):
+            nc.scalar.activation(half_y[:, t, :], y_src[t], ACT.Copy, scale=0.5)
+
+        larger(0)
+        for t in n4_order[:-1]:
+            halve(t)
+        larger(1)
+        halve(n4_order[-1])
+        larger(2)
+        nc.vector.tensor_tensor(st[LAST][:, :S], st[LAST][:, S:], y_bank[LAST][:], ALU.max)
         w3_g = tile("w3_g", [P, PACK * N], BF16)
         deal(nc.scalar.copy, w3_g, w3_raw, 0)
-
-        st = [tile("st%d" % t, [P, WIN], F32) for t in planes]
-        for t in planes:
-            nc.vector.tensor_copy(st[t][:, S:], y[t][:].indirect(n3_t[:]))
-        for t in planes:
-            nc.vector.tensor_tensor(st[t][:, :S], st[t][:, S:], y_bank[t][:], ALU.max)
         gain_y = tile("gain_y", [P, PACK, S], F32)
         for t in planes:
-            nc.scalar.activation(gain_y[:, t, :], y_bank[t][:], ACT.Copy, scale=gn_t[:, t : t + 1])
-        u = tile("u", [P, PACK, S], F32)
-        z2_rows = tile("z2_rows", [P, PACK, S], BF16)
-        for t in planes:
-            nc.vector.tensor_tensor(u[:, t, :], st[t][:].indirect(n4_t[:]), half_y[:, t, :], ALU.subtract)
-            nc.scalar.activation(z2_rows[:, t, :], u[:, t, :], ACT.Copy, scale=gm_t[:, t : t + 1])
-        diff = tile("diff", [P, PACK, S], F32)
+            nc.scalar.activation(gain_y[:, t, :], y_src[t], ACT.Copy, scale=gn_t[:, t : t + 1])
+
+        z2_rows = tile("z2_rows", [P, PACK, S], BF16, tag="z2_then_w2")
+        for t in n4_order:
+            nc.vector.tensor_tensor(ungained[:, t, :], st[t][:].indirect(n4_t[:]), half_y[:, t, :], ALU.subtract)
+            nc.scalar.activation(z2_rows[:, t, :], ungained[:, t, :], ACT.Copy, scale=gm_t[:, t : t + 1])
         z2_g = [diff[:, h, :].bitcast(BF16) for h in range(2)]
         for h in range(2):
             nc.scalar.copy(woven(z2_g[h], 4), unwoven(z2_rows[:, :, halves[h]], 4))
-        w3_q = quantize("w3", w3_g)
-
-        w2_g = tile("w2_g", [P, PACK * N], BF16)
+        w2_g = tile("w2_g", [P, PACK * N], BF16, tag="z2_then_w2")
         deal(nc.scalar.copy, w2_g, w2_raw, 0)
 
-        y_n2 = half_y
-        for t in planes:
-            nc.vector.tensor_copy(y_n2[:, t, :], y[t][:].indirect(n2_t[:]))
+        def difference(t):
+            nc.vector.tensor_tensor(diff[:, t, :], y[t][:].indirect(n1_t[:]), y_n2[:, t, :], ALU.subtract)
+
+        for t in planes[2:]:
+            difference(t)
+        w3_q = quantize("w3", w3_g)
         z2_q = mx_tiles("z2")
         for h in range(2):
             quantize_part(z2_q, halves[h], z2_g[h])
+
         b_bank = [psum.tile([P, S], F32, name="b_bank%d" % t, tag="b%d" % t) for t in planes]
         size_b = [tile("size_b%d" % t, [P, WIN], F32) for t in planes]
         size_own = tile("size_own", [P, PACK, S], F32)
@@ -156,8 +188,8 @@ def tile_picked_forknormbwindhopb_none_p_kernel(tc, x_words, x_scales, w1, gn, w
             nc.scalar.activation(size_b[t][:, :S], b_bank[t][:], ACT.Abs)
             nc.sync.dma_start(out=size_own[:, t, :], in_=size_b[t][:, :S])
 
-        for t in planes:
-            nc.vector.tensor_tensor(diff[:, t, :], y[t][:].indirect(n1_t[:]), y_n2[:, t, :], ALU.subtract)
+        for t in planes[:2]:
+            difference(t)
         w2_q = quantize("w2", w2_g)
         z_g = [tile("z_g%d" % h, [P, PACK * S // 2], BF16) for h in range(2)]
         z_q = mx_tiles("z")
@@ -165,38 +197,42 @@ def tile_picked_forknormbwindhopb_none_p_kernel(tc, x_words, x_scales, w1, gn, w
             nc.vector.tensor_tensor(woven(z_g[h][:], 2), unwoven(diff[:, :, halves[h]], 2), unwoven(gain_y[:, :, halves[h]], 2), ALU.mult)
         for h in range(2):
             quantize_part(z_q, halves[h], z_g[h][:])
+
         a_bank = [psum.tile([P, S], F32, name="a_bank%d" % t, tag="ya%d" % t) for t in planes]
         minus_a = [tile("minus_a%d" % t, [P, WIN], F32) for t in planes]
-        a_own = tile("a_own", [P, PACK, S], F32)
+        minus_own = tile("minus_own", [P, PACK, S], F32)
         for t in planes:
             product(a_bank[t], w2_q, z_q, t)
             nc.scalar.activation(minus_a[t][:, :S], a_bank[t][:], ACT.Copy, scale=-1.0)
-            nc.sync.dma_start(out=a_own[:, t, :], in_=minus_a[t][:, :S])
+            if t > 0:
+                nc.sync.dma_start(out=minus_own[:, t, :], in_=minus_a[t][:, :S])
+        nc.scalar.activation(minus_own[:, 0, :], a_bank[0][:], ACT.Copy, scale=-1.0)
+
         den = tile("den", [P, PACK, S], F32)
         log_den = tile("log_den", [P, PACK, S], F32)
         for t in planes:
             nc.vector.tensor_tensor(den[:, t, :], size_b[t][:].indirect(n6_t[:]), size_own[:, t, :], ALU.add)
             nc.scalar.activation(log_den[:, t, :], den[:, t, :], ACT.Ln, bias=0.5)
-        inv_den = [den[:, PACK - 1, :]] + [log_den[:, t, :] for t in planes[:-1]]
+        inv_den = [den[:, LAST, :]] + [log_den[:, t, :] for t in planes[:LAST]]
         for t in planes:
-            nc.scalar.activation(inv_den[t], log_den[:, t, :], ACT.Exp, scale=-1.0)
+            nc.scalar.activation(inv_den[t], log_den[:, t, :], ACT.Exp, bias=log_one[:], scale=-1.0)
 
-        num = tile("num", [P, PACK - 1, S], F32)
+        num = tile("num", [P, LAST, S], F32)
         res = tile("res", [P, PACK, S], F32)
         out_rows = out.rearrange("(p t) s -> p t s", t=PACK)
 
         def numerator(t):
-            nc.vector.tensor_tensor(num[:, t % 3, :], minus_a[t][:].indirect(n5_t[:]), a_own[:, t, :], ALU.subtract)
+            nc.vector.tensor_tensor(num[:, t % LAST, :], minus_a[t][:].indirect(n5_t[:]), minus_own[:, t, :], ALU.subtract)
 
         def finish(t, places):
-            nc.vector.tensor_tensor(res[:, t, places], num[:, t % 3, places], inv_den[t][:, places], ALU.mult)
+            nc.vector.tensor_tensor(res[:, t, places], num[:, t % LAST, places], inv_den[t][:, places], ALU.mult)
             nc.sync.dma_start(out=out_rows[:, t, places], in_=res[:, t, places])
 
-        for t in range(3):
+        for t in planes[:LAST]:
             numerator(t)
-        finish(0, slice(0, S))
-        finish(1, slice(0, S))
-        numerator(3)
-        finish(2, slice(0, S))
-        finish(3, halves[0])
-        finish(3, halves[1])
+        finish(0, whole)
+        finish(1, whole)
+        numerator(LAST)
+        finish(2, whole)
+        for places in halves:
+            finish(LAST, places)

from contextlib import ExitStack

import concourse.mybir as mybir

K, T, S, H, N = 512, 2048, 512, 512, 512
FLOPS = 2 * K * H * S + 2 * 2 * H * N * S

F32 = mybir.dt.float32
BF16 = mybir.dt.bfloat16
I32 = mybir.dt.int32
U32 = mybir.dt.uint32
U16 = mybir.dt.uint16
U8 = mybir.dt.uint8
FP8X4 = mybir.dt.float8_e4m3fn_x4
ALU = mybir.AluOpType
ACT = mybir.ActivationFunctionType

P = 128
PACK = 4
LIST_ROWS = 16
WIN = 2 * S
LAST = PACK - 1


def tile_picked_forknormbwindhopb_none_p_kernel(tc, x_words, x_scales, w1, gn, w2, gm, w3, offs, n1, n2, n3, n4, n5, n6, out):
    nc = tc.nc
    planes = range(PACK)
    whole = slice(0, S)
    halves = [slice(0, S // 2), slice(S // 2, S)]
    with ExitStack() as ctx:
        keep = ctx.enter_context(tc.tile_pool(name="keep", bufs=1))
        psum = ctx.enter_context(tc.psum_pool(name="psum", bufs=1))

        def tile(name, shape, dtype, tag=None):
            return keep.tile(shape, dtype, name=name, tag=tag or name, align_bytes=64)

        def load_list(name, src):
            dst = tile(name, [P, S // LIST_ROWS], U16)
            nc.sync.dma_start(dst[:], src)
            return dst

        def load_rows(name, w, c0, c1):
            raw = tile(name, [P, PACK, c1 - c0], F32)
            nc.sync.dma_start(out=raw[:], in_=w.rearrange("(p j) c -> p j c", j=PACK)[:, :, c0:c1])
            return raw

        def load_gain(name, g):
            dst = tile(name, [P, PACK], F32)
            nc.sync.dma_start(out=dst[:], in_=g.rearrange("(p t) o -> p (t o)", t=PACK))
            return dst

        def deal(copy, grouped, raw, m0):
            m = raw.shape[2] // PACK
            copy(grouped[:].rearrange("p (t m j) -> p m j t", t=PACK, j=PACK)[:, m0 : m0 + m],
                 raw[:].rearrange("p j (m t) -> p m j t", t=PACK))

        def mx_tiles(name):
            return tile(name + "_codes", [P, S], U32), tile(name + "_scales", [P, S], U8)

        def quantize_part(operand, cols, grouped):
            nc.vector.quantize_mx(out=operand[0][:, cols].bitcast(FP8X4), scales=operand[1][:, cols], in_=grouped)

        def quantize(name, grouped):
            operand = mx_tiles(name)
            quantize_part(operand, whole, grouped[:])
            return operand

        def product(bank, weights, acts, t, places=whole):
            cols = slice(P * t, P * (t + 1))
            nc.tensor.matmul_mx(out=bank[:, places], lhsT=weights[0][:, cols].bitcast(FP8X4), lhsT_scale=weights[1][:, cols],
                                rhs=acts[0][:, places].bitcast(FP8X4), rhs_scale=acts[1][:, places], start=True, stop=True)

        def woven(grouped, i):
            return grouped.rearrange("p (c i t) -> p c t i", i=i, t=PACK)

        def unwoven(rows, i):
            return rows.rearrange("p t (c i) -> p c t i", i=i)

        one = tile("one", [P, 1], F32)
        nc.vector.memset(one[:], 1.0)
        log_one = tile("log_one", [P, 1], F32)
        nc.scalar.activation(log_one[:], one[:], ACT.Ln)

        xs_all = tile("xs_all", [P, T], U8)
        nc.vector.memset(xs_all[:].bitcast(I32), 0)
        w1_lo = load_rows("w1_lo", w1, 0, H // 2)
        for q in range(4):
            nc.sync.dma_start(out=xs_all[32 * q : 32 * q + 4, :].bitcast(I32), in_=x_scales[0, 4 * q : 4 * q + 4, :].bitcast(I32))
        offs_t = load_list("offs_t", offs)
        w1_hi = load_rows("w1_hi", w1, H // 2, H)
        xw_all = tile("xw_all", [P, T], U32)
        nc.sync.dma_start(out=xw_all[:].bitcast(I32), in_=x_words[0].rearrange("p c r -> p (c r)").bitcast(I32))
        n2_t = load_list("n2_t", n2)
        n3_t = load_list("n3_t", n3)
        n4_t = load_list("n4_t", n4)
        gm_t = load_gain("gm_t", gm)
        gn_t = load_gain("gn_t", gn)
        w3_raw = load_rows("w3_raw", w3, 0, N)
        n1_t = load_list("n1_t", n1)
        w2_raw = load_rows("w2_raw", w2, 0, N)
        n6_t = load_list("n6_t", n6)
        n5_t = load_list("n5_t", n5)

        w1_g = tile("w1_g", [P, PACK * H], BF16)
        deal(nc.scalar.copy, w1_g, w1_lo, 0)
        deal(nc.vector.tensor_copy, w1_g, w1_hi, P // 2)
        xs = tile("xs", [P, S], U8)
        nc.vector.tensor_copy(xs[:], xs_all[:].indirect(offs_t[:]))
        w1_q = quantize("w1", w1_g)
        xw = tile("xw", [P, S], U32)
        half_list = S // 2 // LIST_ROWS
        for h in range(2):
            nc.vector.tensor_copy(xw[:, halves[h]], xw_all[:].indirect(offs_t[:, half_list * h : half_list * (h + 1)]))

        y_bank = [psum.tile([P, S], F32, name="y_bank%d" % t, tag="ya%d" % t) for t in planes]
        y = [tile("y%d" % t, [P, WIN], F32) for t in planes]
        y_own = tile("y_own", [P, LAST, S], F32)
        early_bank = psum.tile([P, S], F32, name="early_bank", tag="b%d" % LAST)
        for h, bank in enumerate((early_bank, y_bank[0])):
            product(bank, w1_q, (xw, xs), 0, halves[h])
            nc.scalar.copy(y[0][:, halves[h]], bank[:, halves[h]])
        y_src = [y[0][:, :S]] + [y_bank[t][:] for t in planes[1:]]
        nc.scalar.copy(y_own[:, 0, :], y_src[0])
        for t in planes[1:]:
            product(y_bank[t], w1_q, (xw, xs), t)
            nc.scalar.copy(y[t][:, :S], y_src[t])
            if t < LAST:
                nc.scalar.copy(y_own[:, t, :], y_src[t])

        n4_order = (LAST, 0, 1, 2)
        st = [tile("st%d" % t, [P, PACK * S if t == n4_order[-1] else WIN], F32) for t in planes]
        y_n2 = tile("y_n2", [P, PACK, S], F32)
        ungained = tile("ungained", [P, PACK, S], F32)
        rise = ungained
        for t in planes[:LAST]:
            nc.vector.tensor_copy(y_n2[:, t, :], y[t][:].indirect(n2_t[:]))
            nc.vector.tensor_tensor(st[t][:, S:WIN], y[t][:].indirect(n3_t[:]), y_own[:, t, :], ALU.subtract)
        nc.vector.tensor_copy(st[LAST][:, S:], y[LAST][:].indirect(n3_t[:]))
        nc.vector.tensor_copy(y_n2[:, LAST, :], y[LAST][:].indirect(n2_t[:]))
        diff = st[n4_order[-1]][:].rearrange("p (t s) -> p t s", t=PACK)
        half_y = tile("half_y", [P, PACK, S], F32)

        def larger(t):
            nc.scalar.activation(rise[:, t, :], st[t][:, S:WIN], ACT.Relu)
            nc.gpsimd.tensor_tensor(st[t][:, :S], rise[:, t, :], y_own[:, t, :], ALU.add)

        def halve(t):
            nc.scalar.activation(half_y[:, t, :], y_src[t], ACT.Copy, scale=0.5)

        larger(0)
        for t in n4_order[:-1]:
            halve(t)
        larger(1)
        halve(n4_order[-1])
        larger(2)
        nc.vector.tensor_tensor(st[LAST][:, :S], st[LAST][:, S:], y_bank[LAST][:], ALU.max)
        w3_g = tile("w3_g", [P, PACK * N], BF16)
        deal(nc.scalar.copy, w3_g, w3_raw, 0)
        gain_y = tile("gain_y", [P, PACK, S], F32)
        for t in planes:
            nc.scalar.activation(gain_y[:, t, :], y_src[t], ACT.Copy, scale=gn_t[:, t : t + 1])

        z2_rows = tile("z2_rows", [P, PACK, S], BF16, tag="z2_then_w2")
        for t in n4_order:
            nc.vector.tensor_tensor(ungained[:, t, :], st[t][:].indirect(n4_t[:]), half_y[:, t, :], ALU.subtract)
            nc.scalar.activation(z2_rows[:, t, :], ungained[:, t, :], ACT.Copy, scale=gm_t[:, t : t + 1])
        z2_g = [diff[:, h, :].bitcast(BF16) for h in range(2)]
        for h in range(2):
            nc.scalar.copy(woven(z2_g[h], 4), unwoven(z2_rows[:, :, halves[h]], 4))
        w2_g = tile("w2_g", [P, PACK * N], BF16, tag="z2_then_w2")
        deal(nc.scalar.copy, w2_g, w2_raw, 0)

        def difference(t):
            nc.vector.tensor_tensor(diff[:, t, :], y[t][:].indirect(n1_t[:]), y_n2[:, t, :], ALU.subtract)

        for t in planes[2:]:
            difference(t)
        w3_q = quantize("w3", w3_g)
        z2_q = mx_tiles("z2")
        for h in range(2):
            quantize_part(z2_q, halves[h], z2_g[h])

        b_bank = [psum.tile([P, S], F32, name="b_bank%d" % t, tag="b%d" % t) for t in planes]
        size_b = [tile("size_b%d" % t, [P, WIN], F32) for t in planes]
        size_own = tile("size_own", [P, PACK, S], F32)
        for t in planes:
            product(b_bank[t], w3_q, z2_q, t)
            nc.scalar.activation(size_b[t][:, :S], b_bank[t][:], ACT.Abs)
            nc.sync.dma_start(out=size_own[:, t, :], in_=size_b[t][:, :S])

        for t in planes[:2]:
            difference(t)
        w2_q = quantize("w2", w2_g)
        z_g = [tile("z_g%d" % h, [P, PACK * S // 2], BF16) for h in range(2)]
        z_q = mx_tiles("z")
        for h in range(2):
            nc.vector.tensor_tensor(woven(z_g[h][:], 2), unwoven(diff[:, :, halves[h]], 2), unwoven(gain_y[:, :, halves[h]], 2), ALU.mult)
        for h in range(2):
            quantize_part(z_q, halves[h], z_g[h][:])

        a_bank = [psum.tile([P, S], F32, name="a_bank%d" % t, tag="ya%d" % t) for t in planes]
        minus_a = [tile("minus_a%d" % t, [P, WIN], F32) for t in planes]
        minus_own = tile("minus_own", [P, PACK, S], F32)
        for t in planes:
            product(a_bank[t], w2_q, z_q, t)
            nc.scalar.activation(minus_a[t][:, :S], a_bank[t][:], ACT.Copy, scale=-1.0)
            if t > 0:
                nc.sync.dma_start(out=minus_own[:, t, :], in_=minus_a[t][:, :S])
        nc.scalar.activation(minus_own[:, 0, :], a_bank[0][:], ACT.Copy, scale=-1.0)

        den = tile("den", [P, PACK, S], F32)
        log_den = tile("log_den", [P, PACK, S], F32)
        for t in planes:
            nc.vector.tensor_tensor(den[:, t, :], size_b[t][:].indirect(n6_t[:]), size_own[:, t, :], ALU.add)
            nc.scalar.activation(log_den[:, t, :], den[:, t, :], ACT.Ln, bias=0.5)
        inv_den = [den[:, LAST, :]] + [log_den[:, t, :] for t in planes[:LAST]]
        for t in planes:
            nc.scalar.activation(inv_den[t], log_den[:, t, :], ACT.Exp, bias=log_one[:], scale=-1.0)

        num = tile("num", [P, LAST, S], F32)
        res = tile("res", [P, PACK, S], F32)
        out_rows = out.rearrange("(p t) s -> p t s", t=PACK)

        def numerator(t):
            nc.vector.tensor_tensor(num[:, t % LAST, :], minus_a[t][:].indirect(n5_t[:]), minus_own[:, t, :], ALU.subtract)

        def finish(t, places):
            nc.vector.tensor_tensor(res[:, t, places], num[:, t % LAST, places], inv_den[t][:, places], ALU.mult)
            nc.sync.dma_start(out=out_rows[:, t, places], in_=res[:, t, places])

        for t in planes[:LAST]:
            numerator(t)
        finish(0, whole)
        finish(1, whole)
        numerator(LAST)
        finish(2, whole)
        for places in halves:
            finish(LAST, places)
